import numpy as np
import ml_dtypes


def mxq(x, axis, fmt="e4m3"):
    dtype, down = {"e4m3": (ml_dtypes.float8_e4m3fn, 7), "e5m2": (ml_dtypes.float8_e5m2, 14)}[fmt]
    v = np.moveaxis(np.asarray(x, np.float32).astype(ml_dtypes.bfloat16).astype(np.float64), axis, -1)
    blocks = v.reshape(v.shape[:-1] + (-1, 32))
    amax = np.abs(blocks).max(-1, keepdims=True)
    byte = np.maximum(np.where(amax > 0, np.frexp(amax)[1] - 1 + 127, 0) - down, 1)
    scale = np.exp2(byte - 127.0)
    codes = (blocks / scale).astype(np.float32).astype(dtype).astype(np.float64)
    return np.moveaxis((codes * scale).reshape(v.shape), -1, axis)


WIDE = False


def mx_kscale(k):
    if not WIDE:
        return np.ones(k)
    levels = np.array([10, -10, 5, -5, 0])
    if k % 512:
        return np.exp2(np.random.permutation(np.resize(levels, k // 32))).repeat(32)
    a = np.empty((k // 512, 16))
    for p in range(k // 512):
        a[p, :8] = np.random.permutation(np.resize(levels, 8))
        for g in range(8):
            far = levels[np.abs(levels - a[p, g]) >= 10]
            a[p, g + 8] = far[np.random.randint(len(far))]
    return np.exp2(a.ravel()).repeat(32)


def f64(x):
    return np.asarray(x).astype(np.float64)


def striped(idx):
    return np.tile(idx.reshape(-1, 16).T, (8, 1)).astype(np.uint16)


def unstriped(offs):
    return offs[:16].T.reshape(-1).astype(np.int64)


def striped8(idx):
    return np.concatenate([x.reshape(-1, 16).T for x in idx]).astype(np.uint16)


def runs(offs, k):
    lists = np.stack([offs[16 * r : 16 * r + 16].T.reshape(-1) for r in range(8)]).astype(np.int64)
    return lists[np.arange(k) % 512 // 64]


def pack_weight(w):
    k, n = w.shape
    w = f64(np.asarray(w, np.float32).astype(ml_dtypes.bfloat16)).reshape(k // 32, 32, n)
    amax = np.abs(w).max(1)
    byte = np.clip(np.where(amax > 0, np.frexp(amax)[1] - 1 + 127 - 7, 1), 1, 254)
    scaled = (w * np.exp2(127.0 - byte)[:, None, :]).reshape(k, n).astype(np.float32)
    words = np.ascontiguousarray(scaled.reshape(k // 512, 128, 4, n).transpose(0, 1, 3, 2)).astype(ml_dtypes.float8_e4m3fn).view(np.uint8)
    return words, np.ascontiguousarray(byte.astype(np.uint8).reshape(k // 512, 16, n))


def unpack_weight(words, scales):
    g, p, n, _ = words.shape
    vals = np.ascontiguousarray(words).view(ml_dtypes.float8_e4m3fn).astype(np.float64) * np.repeat(np.exp2(scales.astype(np.float64) - 127.0), 8, axis=1)[..., None]
    return vals.transpose(0, 1, 3, 2).reshape(g * 512, n)


E2M1 = np.array([0.0, 0.5, 1.0, 1.5, 2.0, 3.0, 4.0, 6.0, -0.0, -0.5, -1.0, -1.5, -2.0, -3.0, -4.0, -6.0])


def pack_fp4(w):
    k, n = w.shape
    w = f64(np.asarray(w, np.float32).astype(ml_dtypes.bfloat16)).reshape(k // 32, 32, n)
    amax = np.abs(w).max(1)
    mant, ex = np.frexp(amax / 6.0)
    byte = np.clip(np.where(amax > 0, np.where(mant > 0.5, ex, ex - 1) + 127, 1), 1, 254)
    scaled = (w * np.exp2(127.0 - byte)[:, None, :]).reshape(k, n).astype(np.float32)
    c = np.ascontiguousarray(scaled.reshape(k // 512, 128, 4, n).transpose(0, 1, 3, 2)).astype(ml_dtypes.float4_e2m1fn).view(np.uint8) & 0xF
    words = (c[..., 0::2] | (c[..., 1::2] << 4)).reshape(k // 512, 128, 2 * n)
    return np.ascontiguousarray(words), np.ascontiguousarray(byte.astype(np.uint8).reshape(k // 512, 16, n))


def unpack_fp4(words, scales):
    g, _, n = scales.shape
    words = np.ascontiguousarray(words).reshape(g, 128, n, 2)
    nib = np.empty((g, 128, n, 4), np.uint8)
    nib[..., 0::2] = words & 0xF
    nib[..., 1::2] = words >> 4
    vals = E2M1[nib] * np.repeat(np.exp2(scales.astype(np.float64) - 127.0), 8, axis=1)[..., None]
    return vals.transpose(0, 1, 3, 2).reshape(g * 512, n)


def sigmoid(v):
    return 1.0 / (1.0 + np.exp(-np.maximum(v, -700.0)))

def planes(y):
    n, m = y.shape
    v = y.astype(np.float32).astype(ml_dtypes.bfloat16).astype(np.float64).reshape(n // 32, 32, m)
    top = np.abs(v).max(1)
    byte = np.clip(np.where(top > 0, np.frexp(top)[1] - 1 + 127 - 7, 1), 1, 254)
    codes = (v * np.exp2(127.0 - byte)[:, None, :]).reshape(n, m).astype(np.float32).astype(ml_dtypes.float8_e4m3fn).view(np.uint8)
    words = codes.reshape(n // 512, 128, 4, m).transpose(0, 1, 3, 2)
    return np.ascontiguousarray(words), np.ascontiguousarray(byte.astype(np.uint8).reshape(n // 512, 16, m))


K, T, S, H, U = 512, 2048, 512, 512, 1024


def setup_inputs():
    n = np.random.standard_normal
    s = mx_kscale(K)[:, None]
    u = mx_kscale(S)
    packed_xT = pack_weight(n((K, T)) * s)
    packed_w1 = pack_fp4(n((K, H)) / np.sqrt(K) / s)
    return {
        "x_words": packed_xT[0],
        "x_scales": packed_xT[1],
        "w1_words": packed_w1[0],
        "w1_scales": packed_w1[1],
        "mem": n((H, U)).astype(np.float32),
        "ga": (np.random.uniform(0.5, 1.5, (H, 1)) * u[:, None]).astype(np.float32),
        "gb": (np.random.uniform(0.5, 1.5, (H, 1)) / u[:, None]).astype(np.float32),
        "offs": striped(np.random.permutation(T)[:S]),
        "n1": striped8(np.stack([np.random.permutation(S) for _ in range(8)])),
        "n2": striped8(np.stack([np.random.permutation(S) for _ in range(8)])),
        "n3": striped8(np.stack([np.random.permutation(U)[:S] for _ in range(8)])),
        "n4": striped8(np.stack([np.random.permutation(U) for _ in range(8)])),
        "n5": striped8(np.stack([np.random.permutation(U) for _ in range(8)])),
    }


def reference(x_words, x_scales, w1_words, w1_scales, mem, ga, gb, offs, n1, n2, n3, n4, n5):
    xq = unpack_weight(x_words, x_scales)[:, unstriped(offs)]
    y = unpack_fp4(w1_words, w1_scales).T @ xq
    sq = (y) ** 2
    z = f64(ga) * ((y[np.arange(H)[:, None], runs(n2, H)]) / (np.sqrt(sq + sq[np.arange(H)[:, None], runs(n1, H)] + 0.25)))
    old = f64(mem)[np.arange(H)[:, None], runs(n3, H)]
    nw = old + sigmoid(y) * (y - old)
    pg = f64(mem).copy()
    pg[np.arange(H)[:, None], runs(n3, H)] = nw
    z2 = f64(gb) * pg
    s = 0.0625 * ((mxq(z, 0, "e4m3").T @ mxq(z2, 0, "e4m3")))
    out_0 = (s[np.arange(S)[:, None], runs(n4, S)]) * (s[np.arange(S)[:, None], runs(n5, S)])
    return (out_0,) + planes(out_0)

@@ -1,0 +1,187 @@
+from contextlib import ExitStack
+
+import concourse.mybir as mybir
+
+F32 = mybir.dt.float32
+BF16 = mybir.dt.bfloat16
+I32 = mybir.dt.int32
+U32 = mybir.dt.uint32
+U16 = mybir.dt.uint16
+U8 = mybir.dt.uint8
+FP8X4 = mybir.dt.float8_e4m3fn_x4
+FP4X4 = mybir.dt.float4_e2m1fn_x4
+ACT = mybir.ActivationFunctionType
+MULT = mybir.AluOpType.mult
+ADD = mybir.AluOpType.add
+
+P = 128
+T, S, H, U = 2048, 512, 512, 1024
+FLOPS = 2 * 512 * H * S + 2 * H * S * U
+BANK = 512
+CHUNKS = (512, 256, 128, 128)
+
+
+def tile_picked_selfrmspagetprod_none_po_kernel(
+    tc, x_words, x_scales, w1_words, w1_scales, mem, ga, gb, offs, n1, n2, n3, n4, n5, out_0, out_1, out_2
+):
+    nc = tc.nc
+    with ExitStack() as ctx:
+        lists = ctx.enter_context(tc.tile_pool(name="lists", bufs=1))
+        sb = ctx.enter_context(tc.tile_pool(name="sb", bufs=1))
+        ps = ctx.enter_context(tc.psum_pool(name="ps", bufs=1))
+
+        def tile(name, shape, dtype):
+            return sb.tile([P] + shape, dtype, name=name, align_bytes=64)
+
+        def load_list(name, src):
+            t = lists.tile(list(src.shape), U16, name=name)
+            nc.sync.dma_start(t[:], src)
+            return t
+
+        xs_all = tile("xs_all", [T], U8)
+        ws_raw = tile("ws_raw", [H], U8)
+        nc.gpsimd.memset(ws_raw[:].bitcast(I32), 0)
+        nc.vector.memset(xs_all[:].bitcast(I32), 0)
+        l_offs = load_list("l_offs", offs)
+        ww_raw = tile("ww_raw", [2 * H], U8)
+        nc.sync.dma_start(ww_raw[:].bitcast(I32), w1_words[0].bitcast(I32))
+        for q in range(4):
+            nc.scalar.dma_start(ws_raw[32 * q : 32 * q + 4, :].bitcast(I32), w1_scales[0, 4 * q : 4 * q + 4, :].bitcast(I32))
+        xw_all = tile("xw_all", [T], U32)
+        nc.sync.dma_start(xw_all[:].bitcast(I32), x_words[0].rearrange("p n t -> p (n t)").bitcast(I32))
+        for q in range(4):
+            eng = nc.scalar if q % 2 == 0 else nc.sync
+            eng.dma_start(xs_all[32 * q : 32 * q + 4, :].bitcast(I32), x_scales[0, 4 * q : 4 * q + 4, :].bitcast(I32))
+        l_n3 = load_list("l_n3", n3)
+        page = [tile(f"page{t}", [U], F32) for t in range(4)]
+        mem_t = mem.rearrange("(p t) w -> t p w", t=4)
+        for t in range(4):
+            nc.sync.dma_start(page[t][:], mem_t[t])
+        ga_sb = tile("ga_sb", [4], F32)
+        gb_sb = tile("gb_sb", [4], F32)
+        nc.sync.dma_start(ga_sb[:], ga.rearrange("(p t) o -> p (t o)", t=4))
+        nc.sync.dma_start(gb_sb[:], gb.rearrange("(p t) o -> p (t o)", t=4))
+        l_n1 = load_list("l_n1", n1)
+        l_n2 = load_list("l_n2", n2)
+        l_n4 = load_list("l_n4", n4)
+        l_n5 = load_list("l_n5", n5)
+
+        ww = tile("ww", [2 * H], U8)
+        ws = tile("ws", [H], U8)
+        nc.vector.tensor_copy(
+            ww[:].rearrange("p (t m b) -> p m t b", t=4, b=2), ww_raw[:].rearrange("p (m t b) -> p m t b", t=4, b=2)
+        )
+        nc.vector.tensor_copy(ws[:].rearrange("p (t m) -> p m t", t=4), ws_raw[:].rearrange("p (m t) -> p m t", t=4))
+        xs = tile("xs", [S], U8)
+        xw = tile("xw", [S], U32)
+        nc.vector.tensor_copy(xw[:], xw_all[:].indirect(l_offs[:]))
+        nc.vector.tensor_copy(xs[:], xs_all[:].indirect(l_offs[:]))
+
+        y = [ps.tile([P, BANK], F32, name=f"y{t}", tag=f"bank{t}") for t in range(4)]
+        for t in range(4):
+            nc.tensor.matmul_mx(
+                out=y[t][:],
+                lhsT=ww[:, 2 * P * t : 2 * P * (t + 1)].bitcast(FP4X4),
+                lhsT_scale=ws[:, P * t : P * (t + 1)],
+                rhs=xw[:].bitcast(FP8X4),
+                rhs_scale=xs[:],
+                start=True,
+                stop=True,
+            )
+
+        keep = [tile(f"keep{t}", [S], F32) for t in range(4)]
+        sq_win = [tile(f"sq_win{t}", [2 * S], F32) for t in range(4)]
+        y_win = [tile(f"y_win{t}", [2 * S], F32) for t in range(4)]
+        for t in range(4):
+            nc.scalar.activation(keep[t][:], y[t][:], ACT.Sigmoid, scale=-1.0)
+        for t in range(4):
+            nc.scalar.activation(sq_win[t][:, S:], y[t][:], ACT.Silu)
+        kept = [tile(f"kept{t}", [S], F32) for t in range(4)]
+        for t in range(4):
+            nc.vector.tensor_tensor(kept[t][:], page[t][:].indirect(l_n3[:]), keep[t][:], MULT)
+        for t in range(4):
+            nc.scalar.activation(sq_win[t][:, :S], y[t][:], ACT.Square)
+            nc.scalar.activation(y_win[t][:, S:], y[t][:], ACT.Square)
+            nc.scalar.activation(y_win[t][:, :S], y[t][:], ACT.Copy, scale=ga_sb[:, t : t + 1])
+
+        den = [tile(f"den{t}", [S], F32) for t in range(4)]
+        rstd = [tile(f"rstd{t}", [S], F32) for t in range(4)]
+        z2_rows = tile("z2_rows", [4, U], BF16)
+        for t in range(4):
+            nc.vector.tensor_tensor(page[t][:].indirect(l_n3[:]), kept[t][:], sq_win[t][:, S:], ADD)
+            nc.vector.tensor_tensor(den[t][:], sq_win[t][:].indirect(l_n1[:]), y_win[t][:, S:], ADD)
+            nc.scalar.activation(z2_rows[:, t, :], page[t][:], ACT.Copy, scale=gb_sb[:, t : t + 1])
+            nc.scalar.activation(rstd[t][:], den[t][:], ACT.Abs_reciprocal_sqrt, bias=0.25)
+
+        z2_w = [tile(f"z2_w{h}", [BANK], U32) for h in range(2)]
+        z2_s = [tile(f"z2_s{h}", [BANK], U8) for h in range(2)]
+        z2_in = [tile(f"z2_in{h}", [BANK, 4], BF16) for h in range(2)]
+        for h in range(2):
+            nc.scalar.copy(
+                z2_in[h][:].rearrange("p (c i) t -> p c t i", i=4),
+                z2_rows[:, :, BANK * h : BANK * (h + 1)].rearrange("p t (c i) -> p c t i", i=4),
+            )
+        z_rows = tile("z_rows", [4, S], F32)
+        for t in range(4):
+            nc.vector.tensor_tensor(z_rows[:, t, :], y_win[t][:].indirect(l_n2[:]), rstd[t][:], MULT)
+            if t >= 2:
+                h = t - 2
+                nc.vector.quantize_mx(
+                    out=z2_w[h][:].bitcast(FP8X4), scales=z2_s[h][:], in_=z2_in[h][:].rearrange("p w t -> p (w t)")
+                )
+        z_in = tile("z_in", [4, P, 4], BF16)
+        nc.vector.tensor_copy(
+            z_in[:].rearrange("p u m t -> p m t u"), z_rows[:].rearrange("p t (m u) -> p m t u", u=4)
+        )
+        z_w = tile("z_w", [S], U32)
+        z_s = tile("z_s", [S], U8)
+        nc.vector.quantize_mx(out=z_w[:].bitcast(FP8X4), scales=z_s[:], in_=z_in[:].rearrange("p u m t -> p (u m t)"))
+
+        s_win = [tile(f"s_win{u}", [U], F32) for u in range(4)]
+        first = [tile(f"first{u}", [U], F32) for u in range(4)]
+        for u in range(4):
+            for h in range(2):
+                acc = ps.tile([P, BANK], F32, name=f"s{u}_{h}", tag=f"bank{(4 + 2 * u + h) % 8}")
+                nc.tensor.matmul_mx(
+                    out=acc[:],
+                    lhsT=z_w[:, P * u : P * (u + 1)].bitcast(FP8X4),
+                    lhsT_scale=z_s[:, P * u : P * (u + 1)],
+                    rhs=z2_w[h][:].bitcast(FP8X4),
+                    rhs_scale=z2_s[h][:],
+                    start=True,
+                    stop=True,
+                )
+                nc.scalar.activation(s_win[u][:, BANK * h : BANK * (h + 1)], acc[:], ACT.Copy, scale=0.0625)
+            for h in range(2):
+                nc.vector.tensor_copy(
+                    first[u][:, BANK * h : BANK * (h + 1)], s_win[u][:].indirect(l_n4[:, 32 * h : 32 * (h + 1)])
+                )
+
+        out_rows = out_0.rearrange("(p u) w -> p u w", u=4)
+        out_words = out_1[0].rearrange("p w t -> p (w t)").bitcast(I32)
+        o_s = tile("o_s", [U], U8)
+        c0 = 0
+        for c, width in enumerate(CHUNKS):
+            cols = slice(c0, c0 + width)
+            prod = tile(f"prod{c}", [4, width], F32)
+            for u in range(4):
+                nc.vector.tensor_tensor(
+                    prod[:, u, :], s_win[u][:].indirect(l_n5[:, c0 // 16 : (c0 + width) // 16]), first[u][:, cols], MULT
+                )
+            nc.sync.dma_start(out_rows[:, :, cols], prod[:])
+            o_in = tile(f"o_in{c}", [width, 4], BF16)
+            dst = o_in[:].rearrange("p (c i) u -> p c u i", i=4)
+            src = prod[:].rearrange("p u (c i) -> p c u i", i=4)
+            if c < len(CHUNKS) - 1:
+                nc.scalar.copy(dst, src)
+            else:
+                nc.vector.tensor_copy(dst, src)
+            o_w = tile(f"o_w{c}", [width], U32)
+            nc.vector.quantize_mx(
+                out=o_w[:].bitcast(FP8X4), scales=o_s[:, cols], in_=o_in[:].rearrange("p w u -> p (w u)")
+            )
+            nc.sync.dma_start(out_words[:, cols], o_w[:].bitcast(I32))
+            c0 = c0 + width
+        for q in range(4):
+            eng = nc.scalar if q % 2 == 0 else nc.sync
+            eng.dma_start(out_2[0, 4 * q : 4 * q + 4, :].bitcast(I32), o_s[32 * q : 32 * q + 4, :].bitcast(I32))

@@ -18,7 +18,8 @@ P = 128
 T, S, H, U = 2048, 512, 512, 1024
 FLOPS = 2 * 512 * H * S + 2 * H * S * U
 BANK = 512
-CHUNKS = (512, 256, 128, 128)
+HALF = 256
+CHUNKS = (512, 256, 256)
 
 
 def tile_picked_selfrmspagetprod_none_po_kernel(
@@ -28,6 +29,7 @@ def tile_picked_selfrmspagetprod_none_po_kernel(
     with ExitStack() as ctx:
         lists = ctx.enter_context(tc.tile_pool(name="lists", bufs=1))
         sb = ctx.enter_context(tc.tile_pool(name="sb", bufs=1))
+        ring = ctx.enter_context(tc.tile_pool(name="ring", bufs=2))
         ps = ctx.enter_context(tc.psum_pool(name="ps", bufs=1))
 
         def tile(name, shape, dtype):
@@ -38,27 +40,30 @@ def tile_picked_selfrmspagetprod_none_po_kernel(
             nc.sync.dma_start(t[:], src)
             return t
 
+        def load_scale_rows(eng, dst, src, q):
+            eng.dma_start(dst[32 * q : 32 * q + 4, :].bitcast(I32), src[0, 4 * q : 4 * q + 4, :].bitcast(I32))
+
         xs_all = tile("xs_all", [T], U8)
         ws_raw = tile("ws_raw", [H], U8)
+        ww_raw = tile("ww_raw", [2 * H], U8)
+        xw_all = tile("xw_all", [T], U32)
+        page = [tile(f"page{t}", [U], F32) for t in range(4)]
+        mem_t = mem.rearrange("(p t) w -> t p w", t=4)
+        ga_sb = tile("ga_sb", [4], F32)
+        gb_sb = tile("gb_sb", [4], F32)
         nc.gpsimd.memset(ws_raw[:].bitcast(I32), 0)
         nc.vector.memset(xs_all[:].bitcast(I32), 0)
         l_offs = load_list("l_offs", offs)
-        ww_raw = tile("ww_raw", [2 * H], U8)
         nc.sync.dma_start(ww_raw[:].bitcast(I32), w1_words[0].bitcast(I32))
-        for q in range(4):
-            nc.scalar.dma_start(ws_raw[32 * q : 32 * q + 4, :].bitcast(I32), w1_scales[0, 4 * q : 4 * q + 4, :].bitcast(I32))
-        xw_all = tile("xw_all", [T], U32)
+        load_scale_rows(nc.gpsimd, ws_raw, w1_scales, 3)
+        for q in range(3):
+            load_scale_rows(nc.scalar, ws_raw, w1_scales, q)
         nc.sync.dma_start(xw_all[:].bitcast(I32), x_words[0].rearrange("p n t -> p (n t)").bitcast(I32))
         for q in range(4):
-            eng = nc.scalar if q % 2 == 0 else nc.sync
-            eng.dma_start(xs_all[32 * q : 32 * q + 4, :].bitcast(I32), x_scales[0, 4 * q : 4 * q + 4, :].bitcast(I32))
+            load_scale_rows(nc.sync, xs_all, x_scales, q)
         l_n3 = load_list("l_n3", n3)
-        page = [tile(f"page{t}", [U], F32) for t in range(4)]
-        mem_t = mem.rearrange("(p t) w -> t p w", t=4)
         for t in range(4):
             nc.sync.dma_start(page[t][:], mem_t[t])
-        ga_sb = tile("ga_sb", [4], F32)
-        gb_sb = tile("gb_sb", [4], F32)
         nc.sync.dma_start(ga_sb[:], ga.rearrange("(p t) o -> p (t o)", t=4))
         nc.sync.dma_start(gb_sb[:], gb.rearrange("(p t) o -> p (t o)", t=4))
         l_n1 = load_list("l_n1", n1)
@@ -68,80 +73,104 @@ def tile_picked_selfrmspagetprod_none_po_kernel(
 
         ww = tile("ww", [2 * H], U8)
         ws = tile("ws", [H], U8)
+        xs = tile("xs", [S], U8)
+        xw = tile("xw", [S], U32)
         nc.vector.tensor_copy(
             ww[:].rearrange("p (t m b) -> p m t b", t=4, b=2), ww_raw[:].rearrange("p (m t b) -> p m t b", t=4, b=2)
         )
         nc.vector.tensor_copy(ws[:].rearrange("p (t m) -> p m t", t=4), ws_raw[:].rearrange("p (m t) -> p m t", t=4))
-        xs = tile("xs", [S], U8)
-        xw = tile("xw", [S], U32)
         nc.vector.tensor_copy(xw[:], xw_all[:].indirect(l_offs[:]))
-        nc.vector.tensor_copy(xs[:], xs_all[:].indirect(l_offs[:]))
+        for h in range(2):
+            nc.vector.tensor_copy(xs[:, HALF * h : HALF * (h + 1)], xs_all[:].indirect(l_offs[:, 16 * h : 16 * (h + 1)]))
 
-        y = [ps.tile([P, BANK], F32, name=f"y{t}", tag=f"bank{t}") for t in range(4)]
+        pieces = []
         for t in range(4):
-            nc.tensor.matmul_mx(
-                out=y[t][:],
-                lhsT=ww[:, 2 * P * t : 2 * P * (t + 1)].bitcast(FP4X4),
-                lhsT_scale=ws[:, P * t : P * (t + 1)],
-                rhs=xw[:].bitcast(FP8X4),
-                rhs_scale=xs[:],
-                start=True,
-                stop=True,
-            )
+            for cols in ([slice(0, HALF), slice(HALF, S)] if t == 0 else [slice(0, S)]):
+                n = len(pieces)
+                acc = ps.tile([P, cols.stop - cols.start], F32, name=f"y{n}", tag=f"bank{n}")
+                nc.tensor.matmul_mx(
+                    out=acc[:],
+                    lhsT=ww[:, 2 * P * t : 2 * P * (t + 1)].bitcast(FP4X4),
+                    lhsT_scale=ws[:, P * t : P * (t + 1)],
+                    rhs=xw[:, cols].bitcast(FP8X4),
+                    rhs_scale=xs[:, cols],
+                    start=True,
+                    stop=True,
+                )
+                pieces.append((t, cols, acc))
 
         keep = [tile(f"keep{t}", [S], F32) for t in range(4)]
         sq_win = [tile(f"sq_win{t}", [2 * S], F32) for t in range(4)]
         y_win = [tile(f"y_win{t}", [2 * S], F32) for t in range(4)]
-        for t in range(4):
-            nc.scalar.activation(keep[t][:], y[t][:], ACT.Sigmoid, scale=-1.0)
-        for t in range(4):
-            nc.scalar.activation(sq_win[t][:, S:], y[t][:], ACT.Silu)
         kept = [tile(f"kept{t}", [S], F32) for t in range(4)]
-        for t in range(4):
-            nc.vector.tensor_tensor(kept[t][:], page[t][:].indirect(l_n3[:]), keep[t][:], MULT)
-        for t in range(4):
-            nc.scalar.activation(sq_win[t][:, :S], y[t][:], ACT.Square)
-            nc.scalar.activation(y_win[t][:, S:], y[t][:], ACT.Square)
-            nc.scalar.activation(y_win[t][:, :S], y[t][:], ACT.Copy, scale=ga_sb[:, t : t + 1])
+        for t, cols, acc in pieces:
+            nc.scalar.activation(keep[t][:, cols], acc[:], ACT.Sigmoid, scale=-1.0)
+            nc.vector.tensor_tensor(
+                kept[t][:, cols], page[t][:].indirect(l_n3[:, cols.start // 16 : cols.stop // 16]), keep[t][:, cols], MULT
+            )
+        for t, cols, acc in pieces:
+            nc.scalar.activation(sq_win[t][:, S:][:, cols], acc[:], ACT.Silu)
+        for t, cols, acc in pieces:
+            nc.scalar.activation(sq_win[t][:, cols], acc[:], ACT.Square)
+            nc.scalar.activation(y_win[t][:, S:][:, cols], acc[:], ACT.Square)
+        for t, cols, acc in pieces:
+            nc.scalar.activation(y_win[t][:, cols], acc[:], ACT.Copy, scale=ga_sb[:, t : t + 1])
 
         den = [tile(f"den{t}", [S], F32) for t in range(4)]
         rstd = [tile(f"rstd{t}", [S], F32) for t in range(4)]
         z2_rows = tile("z2_rows", [4, U], BF16)
         for t in range(4):
             nc.vector.tensor_tensor(page[t][:].indirect(l_n3[:]), kept[t][:], sq_win[t][:, S:], ADD)
-            nc.vector.tensor_tensor(den[t][:], sq_win[t][:].indirect(l_n1[:]), y_win[t][:, S:], ADD)
             nc.scalar.activation(z2_rows[:, t, :], page[t][:], ACT.Copy, scale=gb_sb[:, t : t + 1])
-            nc.scalar.activation(rstd[t][:], den[t][:], ACT.Abs_reciprocal_sqrt, bias=0.25)
-
         z2_w = [tile(f"z2_w{h}", [BANK], U32) for h in range(2)]
         z2_s = [tile(f"z2_s{h}", [BANK], U8) for h in range(2)]
         z2_in = [tile(f"z2_in{h}", [BANK, 4], BF16) for h in range(2)]
-        for h in range(2):
-            nc.scalar.copy(
-                z2_in[h][:].rearrange("p (c i) t -> p c t i", i=4),
-                z2_rows[:, :, BANK * h : BANK * (h + 1)].rearrange("p t (c i) -> p c t i", i=4),
+        for t in range(4):
+            nc.vector.tensor_tensor(den[t][:], sq_win[t][:].indirect(l_n1[:]), y_win[t][:, S:], ADD)
+            nc.scalar.activation(rstd[t][:], den[t][:], ACT.Abs_reciprocal_sqrt, bias=0.25)
+            if t in (0, 3):
+                h = t // 3
+                nc.scalar.copy(
+                    z2_in[h][:].rearrange("p (c i) t -> p c t i", i=4),
+                    z2_rows[:, :, BANK * h : BANK * (h + 1)].rearrange("p t (c i) -> p c t i", i=4),
+                )
+
+        def quantize_z2(h):
+            nc.vector.quantize_mx(
+                out=z2_w[h][:].bitcast(FP8X4), scales=z2_s[h][:], in_=z2_in[h][:].rearrange("p w t -> p (w t)")
             )
+
         z_rows = tile("z_rows", [4, S], F32)
         for t in range(4):
             nc.vector.tensor_tensor(z_rows[:, t, :], y_win[t][:].indirect(l_n2[:]), rstd[t][:], MULT)
-            if t >= 2:
-                h = t - 2
-                nc.vector.quantize_mx(
-                    out=z2_w[h][:].bitcast(FP8X4), scales=z2_s[h][:], in_=z2_in[h][:].rearrange("p w t -> p (w t)")
-                )
-        z_in = tile("z_in", [4, P, 4], BF16)
-        nc.vector.tensor_copy(
-            z_in[:].rearrange("p u m t -> p m t u"), z_rows[:].rearrange("p t (m u) -> p m t u", u=4)
-        )
+            if t == 1:
+                quantize_z2(0)
+        z_view = z_rows[:].rearrange("p t (m u) -> p u m t", u=4)
         z_w = tile("z_w", [S], U32)
         z_s = tile("z_s", [S], U8)
-        nc.vector.quantize_mx(out=z_w[:].bitcast(FP8X4), scales=z_s[:], in_=z_in[:].rearrange("p u m t -> p (u m t)"))
+
+        def quantize_z(z_in, u0, u1):
+            nc.vector.quantize_mx(
+                out=z_w[:, P * u0 : P * u1].bitcast(FP8X4),
+                scales=z_s[:, P * u0 : P * u1],
+                in_=z_in.rearrange("p u m t -> p (u m t)"),
+            )
+
+        z_first = tile("z_first", [1, P, 4], BF16)
+        nc.vector.tensor_copy(z_first[:], z_view[:, 0:1])
+        quantize_z(z_first[:], 0, 1)
+        quantize_z2(1)
+        z_rest = sb.tile([P, 3, P, 4], BF16, name="z_rest", tag="z2_in1", align_bytes=64)
+        nc.vector.tensor_copy(
+            z_rest[:].rearrange("p u m t -> p m t u"), z_view[:, 1:4].rearrange("p u m t -> p m t u")
+        )
+        quantize_z(z_rest[:, 0:1], 1, 2)
+        quantize_z(z_rest[:, 1:3], 2, 4)
 
         s_win = [tile(f"s_win{u}", [U], F32) for u in range(4)]
-        first = [tile(f"first{u}", [U], F32) for u in range(4)]
         for u in range(4):
             for h in range(2):
-                acc = ps.tile([P, BANK], F32, name=f"s{u}_{h}", tag=f"bank{(4 + 2 * u + h) % 8}")
+                acc = ps.tile([P, BANK], F32, name=f"s{u}_{h}", tag=f"bank{(5 + 2 * u + h) % 8}")
                 nc.tensor.matmul_mx(
                     out=acc[:],
                     lhsT=z_w[:, P * u : P * (u + 1)].bitcast(FP8X4),
@@ -152,36 +181,55 @@ def tile_picked_selfrmspagetprod_none_po_kernel(
                     stop=True,
                 )
                 nc.scalar.activation(s_win[u][:, BANK * h : BANK * (h + 1)], acc[:], ACT.Copy, scale=0.0625)
-            for h in range(2):
-                nc.vector.tensor_copy(
-                    first[u][:, BANK * h : BANK * (h + 1)], s_win[u][:].indirect(l_n4[:, 32 * h : 32 * (h + 1)])
-                )
 
         out_rows = out_0.rearrange("(p u) w -> p u w", u=4)
         out_words = out_1[0].rearrange("p w t -> p (w t)").bitcast(I32)
         o_s = tile("o_s", [U], U8)
-        c0 = 0
-        for c, width in enumerate(CHUNKS):
-            cols = slice(c0, c0 + width)
-            prod = tile(f"prod{c}", [4, width], F32)
-            for u in range(4):
-                nc.vector.tensor_tensor(
-                    prod[:, u, :], s_win[u][:].indirect(l_n5[:, c0 // 16 : (c0 + width) // 16]), first[u][:, cols], MULT
-                )
-            nc.sync.dma_start(out_rows[:, :, cols], prod[:])
-            o_in = tile(f"o_in{c}", [width, 4], BF16)
-            dst = o_in[:].rearrange("p (c i) u -> p c u i", i=4)
-            src = prod[:].rearrange("p u (c i) -> p c u i", i=4)
-            if c < len(CHUNKS) - 1:
-                nc.scalar.copy(dst, src)
-            else:
-                nc.vector.tensor_copy(dst, src)
-            o_w = tile(f"o_w{c}", [width], U32)
-            nc.vector.quantize_mx(
-                out=o_w[:].bitcast(FP8X4), scales=o_s[:, cols], in_=o_in[:].rearrange("p w u -> p (w u)")
+        o_w = tile("o_w", [U], U32)
+        starts = [sum(CHUNKS[:c]) for c in range(len(CHUNKS))]
+        prod = [tile(f"prod{c}", [4, width], F32) for c, width in enumerate(CHUNKS)]
+        steps = [(c, u) for c in range(len(CHUNKS)) for u in range(4)]
+        first = {}
+
+        def fetch_first(c, u):
+            first[c, u] = ring.tile([P, CHUNKS[c]], F32, name=f"first{c}_{u}", tag="first")
+            nc.vector.tensor_copy(
+                first[c, u][:], s_win[u][:].indirect(l_n4[:, starts[c] // 16 : (starts[c] + CHUNKS[c]) // 16])
             )
-            nc.sync.dma_start(out_words[:, cols], o_w[:].bitcast(I32))
-            c0 = c0 + width
+
+        def regroup(eng_copy, c, a, b):
+            o_in = tile(f"o_in{c}_{a}", [b - a, 4], BF16)
+            eng_copy(
+                o_in[:].rearrange("p (c i) u -> p c u i", i=4), prod[c][:, :, a:b].rearrange("p u (c i) -> p c u i", i=4)
+            )
+            return o_in
+
+        def quantize_out(o_in, cols):
+            nc.vector.quantize_mx(
+                out=o_w[:, cols].bitcast(FP8X4), scales=o_s[:, cols], in_=o_in[:].rearrange("p w u -> p (w u)")
+            )
+
+        waiting = None
+        fetch_first(*steps[0])
+        for n, (c, u) in enumerate(steps):
+            cols = slice(starts[c], starts[c] + CHUNKS[c])
+            if n + 1 < len(steps):
+                fetch_first(*steps[n + 1])
+            nc.vector.tensor_tensor(
+                prod[c][:, u, :], s_win[u][:].indirect(l_n5[:, cols.start // 16 : cols.stop // 16]), first[c, u][:], MULT
+            )
+            nc.sync.dma_start(out_rows[:, u, cols], prod[c][:, u, :])
+            if u == 2 and waiting is not None:
+                quantize_out(*waiting)
+                nc.sync.dma_start(out_words[:, waiting[1]], o_w[:, waiting[1]].bitcast(I32))
+            if u == 3 and c < len(CHUNKS) - 1:
+                waiting = (regroup(nc.scalar.copy, c, 0, CHUNKS[c]), cols)
+        half = CHUNKS[-1] // 2
+        in_a = regroup(nc.vector.tensor_copy, len(CHUNKS) - 1, 0, half)
+        in_b = regroup(nc.scalar.copy, len(CHUNKS) - 1, half, 2 * half)
+        quantize_out(in_a, slice(starts[-1], starts[-1] + half))
+        quantize_out(in_b, slice(starts[-1] + half, U))
+        nc.scalar.dma_start(out_words[:, starts[-1] :], o_w[:, starts[-1] :].bitcast(I32))
         for q in range(4):
-            eng = nc.scalar if q % 2 == 0 else nc.sync
+            eng = nc.scalar if q % 2 == 1 else nc.sync
             eng.dma_start(out_2[0, 4 * q : 4 * q + 4, :].bitcast(I32), o_s[32 * q : 32 * q + 4, :].bitcast(I32))

@@ -29,7 +29,6 @@ def tile_picked_selfrmspagetprod_none_po_kernel(
     with ExitStack() as ctx:
         lists = ctx.enter_context(tc.tile_pool(name="lists", bufs=1))
         sb = ctx.enter_context(tc.tile_pool(name="sb", bufs=1))
-        ring = ctx.enter_context(tc.tile_pool(name="ring", bufs=2))
         ps = ctx.enter_context(tc.psum_pool(name="ps", bufs=1))
 
         def tile(name, shape, dtype):
@@ -55,12 +54,11 @@ def tile_picked_selfrmspagetprod_none_po_kernel(
         nc.vector.memset(xs_all[:].bitcast(I32), 0)
         l_offs = load_list("l_offs", offs)
         nc.sync.dma_start(ww_raw[:].bitcast(I32), w1_words[0].bitcast(I32))
-        load_scale_rows(nc.gpsimd, ws_raw, w1_scales, 3)
-        for q in range(3):
-            load_scale_rows(nc.scalar, ws_raw, w1_scales, q)
+        for q in range(4):
+            load_scale_rows(nc.sync if q < 2 else nc.scalar, xs_all, x_scales, q)
         nc.sync.dma_start(xw_all[:].bitcast(I32), x_words[0].rearrange("p n t -> p (n t)").bitcast(I32))
         for q in range(4):
-            load_scale_rows(nc.sync, xs_all, x_scales, q)
+            load_scale_rows(nc.sync, ws_raw, w1_scales, q)
         l_n3 = load_list("l_n3", n3)
         for t in range(4):
             nc.sync.dma_start(page[t][:], mem_t[t])
@@ -78,10 +76,10 @@ def tile_picked_selfrmspagetprod_none_po_kernel(
         nc.vector.tensor_copy(
             ww[:].rearrange("p (t m b) -> p m t b", t=4, b=2), ww_raw[:].rearrange("p (m t b) -> p m t b", t=4, b=2)
         )
+        nc.vector.tensor_copy(xs[:], xs_all[:].indirect(l_offs[:]))
+        nc.vector.tensor_copy(xw[:, :HALF], xw_all[:].indirect(l_offs[:, :16]))
         nc.vector.tensor_copy(ws[:].rearrange("p (t m) -> p m t", t=4), ws_raw[:].rearrange("p (m t) -> p m t", t=4))
-        nc.vector.tensor_copy(xw[:], xw_all[:].indirect(l_offs[:]))
-        for h in range(2):
-            nc.vector.tensor_copy(xs[:, HALF * h : HALF * (h + 1)], xs_all[:].indirect(l_offs[:, 16 * h : 16 * (h + 1)]))
+        nc.vector.tensor_copy(xw[:, HALF:], xw_all[:].indirect(l_offs[:, 16:]))
 
         pieces = []
         for t in range(4):
@@ -187,15 +185,28 @@ def tile_picked_selfrmspagetprod_none_po_kernel(
         o_s = tile("o_s", [U], U8)
         o_w = tile("o_w", [U], U32)
         starts = [sum(CHUNKS[:c]) for c in range(len(CHUNKS))]
-        prod = [tile(f"prod{c}", [4, width], F32) for c, width in enumerate(CHUNKS)]
-        steps = [(c, u) for c in range(len(CHUNKS)) for u in range(4)]
-        first = {}
 
-        def fetch_first(c, u):
-            first[c, u] = ring.tile([P, CHUNKS[c]], F32, name=f"first{c}_{u}", tag="first")
-            nc.vector.tensor_copy(
-                first[c, u][:], s_win[u][:].indirect(l_n4[:, starts[c] // 16 : (starts[c] + CHUNKS[c]) // 16])
+        def fetch_first(dst, c, u):
+            nc.vector.tensor_copy(dst, s_win[u][:].indirect(l_n4[:, starts[c] // 16 : (starts[c] + CHUNKS[c]) // 16]))
+
+        def product(dst, c, u, first):
+            cols = slice(starts[c], starts[c] + CHUNKS[c])
+            nc.vector.tensor_tensor(
+                dst[:, u, :], s_win[u][:].indirect(l_n5[:, cols.start // 16 : cols.stop // 16]), first, MULT
             )
+            nc.sync.dma_start(out_rows[:, u, cols], dst[:, u, :])
+
+        first_a = [tile(f"first_a{u}", [CHUNKS[0]], F32) for u in range(4)]
+        first_b = tile("first_b", [4, CHUNKS[1]], F32)
+        prod_a = tile("prod_a", [4, CHUNKS[0]], F32)
+        for u in range(4):
+            fetch_first(first_a[u][:], 0, u)
+            fetch_first(first_b[:, u, :], 1, u)
+            product(prod_a, 0, u, first_a[u][:])
+        later = sb.tile([P, 2, 4, HALF], F32, name="later", tag="first_a3", align_bytes=64)
+        prod_c = tile("prod_c", [4, CHUNKS[2]], F32)
+        prod = [prod_a, later[:, 0], prod_c]
+        first_c = later[:, 1]
 
         def regroup(eng_copy, c, a, b):
             o_in = tile(f"o_in{c}_{a}", [b - a, 4], BF16)
@@ -209,21 +220,20 @@ def tile_picked_selfrmspagetprod_none_po_kernel(
                 out=o_w[:, cols].bitcast(FP8X4), scales=o_s[:, cols], in_=o_in[:].rearrange("p w u -> p (w u)")
             )
 
-        waiting = None
-        fetch_first(*steps[0])
-        for n, (c, u) in enumerate(steps):
+        def finish(o_in, c):
             cols = slice(starts[c], starts[c] + CHUNKS[c])
-            if n + 1 < len(steps):
-                fetch_first(*steps[n + 1])
-            nc.vector.tensor_tensor(
-                prod[c][:, u, :], s_win[u][:].indirect(l_n5[:, cols.start // 16 : cols.stop // 16]), first[c, u][:], MULT
-            )
-            nc.sync.dma_start(out_rows[:, u, cols], prod[c][:, u, :])
-            if u == 2 and waiting is not None:
-                quantize_out(*waiting)
-                nc.sync.dma_start(out_words[:, waiting[1]], o_w[:, waiting[1]].bitcast(I32))
-            if u == 3 and c < len(CHUNKS) - 1:
-                waiting = (regroup(nc.scalar.copy, c, 0, CHUNKS[c]), cols)
+            quantize_out(o_in, cols)
+            nc.sync.dma_start(out_words[:, cols], o_w[:, cols].bitcast(I32))
+
+        in_0 = regroup(nc.scalar.copy, 0, 0, CHUNKS[0])
+        for u in range(4):
+            fetch_first(first_c[:, u, :], 2, u)
+            product(prod[1], 1, u, first_b[:, u, :])
+        finish(in_0, 0)
+        in_1 = regroup(nc.scalar.copy, 1, 0, CHUNKS[1])
+        for u in range(4):
+            product(prod[2], 2, u, first_c[:, u, :])
+        finish(in_1, 1)
         half = CHUNKS[-1] // 2
         in_a = regroup(nc.vector.tensor_copy, len(CHUNKS) - 1, 0, half)
         in_b = regroup(nc.scalar.copy, len(CHUNKS) - 1, half, 2 * half)

@@ -72,29 +72,32 @@ def tile_picked_selfrmspagetprod_none_po_kernel(
         ww = tile("ww", [2 * H], U8)
         ws = tile("ws", [H], U8)
         xs = tile("xs", [S], U8)
-        xw = tile("xw", [S], U32)
+        xw_a = tile("xw_a", [HALF], U32)
         nc.vector.tensor_copy(
             ww[:].rearrange("p (t m b) -> p m t b", t=4, b=2), ww_raw[:].rearrange("p (m t b) -> p m t b", t=4, b=2)
         )
         nc.vector.tensor_copy(xs[:], xs_all[:].indirect(l_offs[:]))
-        nc.vector.tensor_copy(xw[:, :HALF], xw_all[:].indirect(l_offs[:, :16]))
+        nc.vector.tensor_copy(xw_a[:], xw_all[:].indirect(l_offs[:, :16]))
         nc.vector.tensor_copy(ws[:].rearrange("p (t m) -> p m t", t=4), ws_raw[:].rearrange("p (m t) -> p m t", t=4))
-        nc.vector.tensor_copy(xw[:, HALF:], xw_all[:].indirect(l_offs[:, 16:]))
+        xw_b = sb.tile([P, HALF], U32, name="xw_b", tag="ws_raw", align_bytes=64)
+        nc.vector.tensor_copy(xw_b[:], xw_all[:].indirect(l_offs[:, 16:]))
+        xw = [xw_a, xw_b]
 
         pieces = []
         for t in range(4):
             for cols in ([slice(0, HALF), slice(HALF, S)] if t == 0 else [slice(0, S)]):
                 n = len(pieces)
                 acc = ps.tile([P, cols.stop - cols.start], F32, name=f"y{n}", tag=f"bank{n}")
-                nc.tensor.matmul_mx(
-                    out=acc[:],
-                    lhsT=ww[:, 2 * P * t : 2 * P * (t + 1)].bitcast(FP4X4),
-                    lhsT_scale=ws[:, P * t : P * (t + 1)],
-                    rhs=xw[:, cols].bitcast(FP8X4),
-                    rhs_scale=xs[:, cols],
-                    start=True,
-                    stop=True,
-                )
+                for h in range(cols.start // HALF, cols.stop // HALF):
+                    nc.tensor.matmul_mx(
+                        out=acc[:, HALF * h - cols.start : HALF * (h + 1) - cols.start],
+                        lhsT=ww[:, 2 * P * t : 2 * P * (t + 1)].bitcast(FP4X4),
+                        lhsT_scale=ws[:, P * t : P * (t + 1)],
+                        rhs=xw[h][:].bitcast(FP8X4),
+                        rhs_scale=xs[:, HALF * h : HALF * (h + 1)],
+                        start=True,
+                        stop=True,
+                    )
                 pieces.append((t, cols, acc))
 
         keep = [tile(f"keep{t}", [S], F32) for t in range(4)]
@@ -106,32 +109,65 @@ def tile_picked_selfrmspagetprod_none_po_kernel(
             nc.vector.tensor_tensor(
                 kept[t][:, cols], page[t][:].indirect(l_n3[:, cols.start // 16 : cols.stop // 16]), keep[t][:, cols], MULT
             )
-        for t, cols, acc in pieces:
-            nc.scalar.activation(sq_win[t][:, S:][:, cols], acc[:], ACT.Silu)
-        for t, cols, acc in pieces:
-            nc.scalar.activation(sq_win[t][:, cols], acc[:], ACT.Square)
-            nc.scalar.activation(y_win[t][:, S:][:, cols], acc[:], ACT.Square)
-        for t, cols, acc in pieces:
-            nc.scalar.activation(y_win[t][:, cols], acc[:], ACT.Copy, scale=ga_sb[:, t : t + 1])
+
+        def from_y(func, dst, ts, **kw):
+            for t, cols, acc in pieces:
+                if t in ts:
+                    nc.scalar.activation(dst(t)[:, cols], acc[:], func, **kw)
+
+        def squares(t):
+            from_y(ACT.Square, lambda t: sq_win[t][:, :S], [t])
+            from_y(ACT.Square, lambda t: y_win[t][:, S:], [t])
+
+        def weighted(t):
+            from_y(ACT.Copy, lambda t: y_win[t][:, :S], [t], scale=ga_sb[:, t : t + 1])
 
         den = [tile(f"den{t}", [S], F32) for t in range(4)]
         rstd = [tile(f"rstd{t}", [S], F32) for t in range(4)]
         z2_rows = tile("z2_rows", [4, U], BF16)
-        for t in range(4):
-            nc.vector.tensor_tensor(page[t][:].indirect(l_n3[:]), kept[t][:], sq_win[t][:, S:], ADD)
-            nc.scalar.activation(z2_rows[:, t, :], page[t][:], ACT.Copy, scale=gb_sb[:, t : t + 1])
         z2_w = [tile(f"z2_w{h}", [BANK], U32) for h in range(2)]
         z2_s = [tile(f"z2_s{h}", [BANK], U8) for h in range(2)]
         z2_in = [tile(f"z2_in{h}", [BANK, 4], BF16) for h in range(2)]
-        for t in range(4):
+
+        def put(t):
+            nc.vector.tensor_tensor(page[t][:].indirect(l_n3[:]), kept[t][:], sq_win[t][:, S:], ADD)
+
+        def round_page(t):
+            nc.scalar.activation(z2_rows[:, t, :], page[t][:], ACT.Copy, scale=gb_sb[:, t : t + 1])
+
+        def denominator(t):
             nc.vector.tensor_tensor(den[t][:], sq_win[t][:].indirect(l_n1[:]), y_win[t][:, S:], ADD)
+
+        def inverse_root(t):
             nc.scalar.activation(rstd[t][:], den[t][:], ACT.Abs_reciprocal_sqrt, bias=0.25)
-            if t in (0, 3):
-                h = t // 3
-                nc.scalar.copy(
-                    z2_in[h][:].rearrange("p (c i) t -> p c t i", i=4),
-                    z2_rows[:, :, BANK * h : BANK * (h + 1)].rearrange("p t (c i) -> p c t i", i=4),
-                )
+
+        def regroup_z2(h):
+            nc.scalar.copy(
+                z2_in[h][:].rearrange("p (c i) t -> p c t i", i=4),
+                z2_rows[:, :, BANK * h : BANK * (h + 1)].rearrange("p t (c i) -> p c t i", i=4),
+            )
+
+        from_y(ACT.Silu, lambda t: sq_win[t][:, S:], [0, 1, 2])
+        for t in range(2):
+            squares(t)
+        from_y(ACT.Silu, lambda t: sq_win[t][:, S:], [3])
+        for t in range(2, 4):
+            squares(t)
+        for t in range(4):
+            weighted(t)
+        for t in range(3):
+            put(t)
+            round_page(t)
+        for t in range(2):
+            denominator(t)
+            inverse_root(t)
+        put(3)
+        round_page(3)
+        regroup_z2(0)
+        for t in range(2, 4):
+            denominator(t)
+            inverse_root(t)
+        regroup_z2(1)
 
         def quantize_z2(h):
             nc.vector.quantize_mx(

from contextlib import ExitStack

import concourse.mybir as mybir

F32 = mybir.dt.float32
BF16 = mybir.dt.bfloat16
I32 = mybir.dt.int32
U32 = mybir.dt.uint32
U16 = mybir.dt.uint16
U8 = mybir.dt.uint8
FP8X4 = mybir.dt.float8_e4m3fn_x4
FP4X4 = mybir.dt.float4_e2m1fn_x4
ACT = mybir.ActivationFunctionType
MULT = mybir.AluOpType.mult
ADD = mybir.AluOpType.add

P = 128
T, S, H, U = 2048, 512, 512, 1024
FLOPS = 2 * 512 * H * S + 2 * H * S * U
BANK = 512
HALF = 256
CHUNKS = (512, 256, 256)


def tile_picked_selfrmspagetprod_none_po_kernel(
    tc, x_words, x_scales, w1_words, w1_scales, mem, ga, gb, offs, n1, n2, n3, n4, n5, out_0, out_1, out_2
):
    nc = tc.nc
    with ExitStack() as ctx:
        lists = ctx.enter_context(tc.tile_pool(name="lists", bufs=1))
        sb = ctx.enter_context(tc.tile_pool(name="sb", bufs=1))
        ps = ctx.enter_context(tc.psum_pool(name="ps", bufs=1))

        def tile(name, shape, dtype):
            return sb.tile([P] + shape, dtype, name=name, align_bytes=64)

        def load_list(name, src):
            t = lists.tile(list(src.shape), U16, name=name)
            nc.sync.dma_start(t[:], src)
            return t

        def load_scale_rows(eng, dst, src, q):
            eng.dma_start(dst[32 * q : 32 * q + 4, :].bitcast(I32), src[0, 4 * q : 4 * q + 4, :].bitcast(I32))

        xs_all = tile("xs_all", [T], U8)
        ws_raw = tile("ws_raw", [H], U8)
        ww_raw = tile("ww_raw", [2 * H], U8)
        xw_all = tile("xw_all", [T], U32)
        page = [tile(f"page{t}", [U], F32) for t in range(4)]
        mem_t = mem.rearrange("(p t) w -> t p w", t=4)
        ga_sb = tile("ga_sb", [4], F32)
        gb_sb = tile("gb_sb", [4], F32)
        nc.gpsimd.memset(ws_raw[:].bitcast(I32), 0)
        nc.vector.memset(xs_all[:].bitcast(I32), 0)
        l_offs = load_list("l_offs", offs)
        nc.sync.dma_start(ww_raw[:].bitcast(I32), w1_words[0].bitcast(I32))
        for q in range(4):
            load_scale_rows(nc.sync if q < 2 else nc.scalar, xs_all, x_scales, q)
        nc.sync.dma_start(xw_all[:].bitcast(I32), x_words[0].rearrange("p n t -> p (n t)").bitcast(I32))
        for q in range(4):
            load_scale_rows(nc.sync, ws_raw, w1_scales, q)
        l_n3 = load_list("l_n3", n3)
        for t in range(4):
            nc.sync.dma_start(page[t][:], mem_t[t])
        nc.sync.dma_start(ga_sb[:], ga.rearrange("(p t) o -> p (t o)", t=4))
        nc.sync.dma_start(gb_sb[:], gb.rearrange("(p t) o -> p (t o)", t=4))
        l_n1 = load_list("l_n1", n1)
        l_n2 = load_list("l_n2", n2)
        l_n4 = load_list("l_n4", n4)
        l_n5 = load_list("l_n5", n5)

        ww = tile("ww", [2 * H], U8)
        ws = tile("ws", [H], U8)
        xs = tile("xs", [S], U8)
        xw_a = tile("xw_a", [HALF], U32)
        nc.vector.tensor_copy(
            ww[:].rearrange("p (t m b) -> p m t b", t=4, b=2), ww_raw[:].rearrange("p (m t b) -> p m t b", t=4, b=2)
        )
        nc.vector.tensor_copy(xs[:], xs_all[:].indirect(l_offs[:]))
        nc.vector.tensor_copy(xw_a[:], xw_all[:].indirect(l_offs[:, :16]))
        nc.vector.tensor_copy(ws[:].rearrange("p (t m) -> p m t", t=4), ws_raw[:].rearrange("p (m t) -> p m t", t=4))
        xw_b = sb.tile([P, HALF], U32, name="xw_b", tag="ws_raw", align_bytes=64)
        nc.vector.tensor_copy(xw_b[:], xw_all[:].indirect(l_offs[:, 16:]))
        xw = [xw_a, xw_b]

        pieces = []
        for t in range(4):
            for cols in ([slice(0, HALF), slice(HALF, S)] if t == 0 else [slice(0, S)]):
                n = len(pieces)
                acc = ps.tile([P, cols.stop - cols.start], F32, name=f"y{n}", tag=f"bank{n}")
                for h in range(cols.start // HALF, cols.stop // HALF):
                    nc.tensor.matmul_mx(
                        out=acc[:, HALF * h - cols.start : HALF * (h + 1) - cols.start],
                        lhsT=ww[:, 2 * P * t : 2 * P * (t + 1)].bitcast(FP4X4),
                        lhsT_scale=ws[:, P * t : P * (t + 1)],
                        rhs=xw[h][:].bitcast(FP8X4),
                        rhs_scale=xs[:, HALF * h : HALF * (h + 1)],
                        start=True,
                        stop=True,
                    )
                pieces.append((t, cols, acc))

        keep = [tile(f"keep{t}", [S], F32) for t in range(4)]
        sq_win = [tile(f"sq_win{t}", [2 * S], F32) for t in range(4)]
        y_win = [tile(f"y_win{t}", [2 * S], F32) for t in range(4)]
        kept = [tile(f"kept{t}", [S], F32) for t in range(4)]
        for t, cols, acc in pieces:
            nc.scalar.activation(keep[t][:, cols], acc[:], ACT.Sigmoid, scale=-1.0)
            nc.vector.tensor_tensor(
                kept[t][:, cols], page[t][:].indirect(l_n3[:, cols.start // 16 : cols.stop // 16]), keep[t][:, cols], MULT
            )

        def from_y(func, dst, ts, **kw):
            for t, cols, acc in pieces:
                if t in ts:
                    nc.scalar.activation(dst(t)[:, cols], acc[:], func, **kw)

        def squares(t):
            from_y(ACT.Square, lambda t: sq_win[t][:, :S], [t])
            from_y(ACT.Square, lambda t: y_win[t][:, S:], [t])

        def weighted(t):
            from_y(ACT.Copy, lambda t: y_win[t][:, :S], [t], scale=ga_sb[:, t : t + 1])

        den = [tile(f"den{t}", [S], F32) for t in range(4)]
        rstd = [tile(f"rstd{t}", [S], F32) for t in range(4)]
        z2_rows = tile("z2_rows", [4, U], BF16)
        z2_w = [tile(f"z2_w{h}", [BANK], U32) for h in range(2)]
        z2_s = [tile(f"z2_s{h}", [BANK], U8) for h in range(2)]
        z2_in = [tile(f"z2_in{h}", [BANK, 4], BF16) for h in range(2)]

        def put(t):
            nc.vector.tensor_tensor(page[t][:].indirect(l_n3[:]), kept[t][:], sq_win[t][:, S:], ADD)

        def round_page(t):
            nc.scalar.activation(z2_rows[:, t, :], page[t][:], ACT.Copy, scale=gb_sb[:, t : t + 1])

        def denominator(t):
            nc.vector.tensor_tensor(den[t][:], sq_win[t][:].indirect(l_n1[:]), y_win[t][:, S:], ADD)

        def inverse_root(t):
            nc.scalar.activation(rstd[t][:], den[t][:], ACT.Abs_reciprocal_sqrt, bias=0.25)

        def regroup_z2(h):
            nc.scalar.copy(
                z2_in[h][:].rearrange("p (c i) t -> p c t i", i=4),
                z2_rows[:, :, BANK * h : BANK * (h + 1)].rearrange("p t (c i) -> p c t i", i=4),
            )

        from_y(ACT.Silu, lambda t: sq_win[t][:, S:], [0, 1, 2])
        for t in range(2):
            squares(t)
        from_y(ACT.Silu, lambda t: sq_win[t][:, S:], [3])
        for t in range(2, 4):
            squares(t)
        for t in range(4):
            weighted(t)
        for t in range(3):
            put(t)
            round_page(t)
        for t in range(2):
            denominator(t)
            inverse_root(t)
        put(3)
        round_page(3)
        regroup_z2(0)
        for t in range(2, 4):
            denominator(t)
            inverse_root(t)
        regroup_z2(1)

        def quantize_z2(h):
            nc.vector.quantize_mx(
                out=z2_w[h][:].bitcast(FP8X4), scales=z2_s[h][:], in_=z2_in[h][:].rearrange("p w t -> p (w t)")
            )

        z_rows = tile("z_rows", [4, S], F32)
        for t in range(4):
            nc.vector.tensor_tensor(z_rows[:, t, :], y_win[t][:].indirect(l_n2[:]), rstd[t][:], MULT)
            if t == 1:
                quantize_z2(0)
        z_view = z_rows[:].rearrange("p t (m u) -> p u m t", u=4)
        z_w = tile("z_w", [S], U32)
        z_s = tile("z_s", [S], U8)

        def quantize_z(z_in, u0, u1):
            nc.vector.quantize_mx(
                out=z_w[:, P * u0 : P * u1].bitcast(FP8X4),
                scales=z_s[:, P * u0 : P * u1],
                in_=z_in.rearrange("p u m t -> p (u m t)"),
            )

        z_first = tile("z_first", [1, P, 4], BF16)
        nc.vector.tensor_copy(z_first[:], z_view[:, 0:1])
        quantize_z(z_first[:], 0, 1)
        quantize_z2(1)
        z_rest = sb.tile([P, 3, P, 4], BF16, name="z_rest", tag="z2_in1", align_bytes=64)
        nc.vector.tensor_copy(
            z_rest[:].rearrange("p u m t -> p m t u"), z_view[:, 1:4].rearrange("p u m t -> p m t u")
        )
        quantize_z(z_rest[:, 0:1], 1, 2)
        quantize_z(z_rest[:, 1:3], 2, 4)

        s_win = [tile(f"s_win{u}", [U], F32) for u in range(4)]
        for u in range(4):
            for h in range(2):
                acc = ps.tile([P, BANK], F32, name=f"s{u}_{h}", tag=f"bank{(5 + 2 * u + h) % 8}")
                nc.tensor.matmul_mx(
                    out=acc[:],
                    lhsT=z_w[:, P * u : P * (u + 1)].bitcast(FP8X4),
                    lhsT_scale=z_s[:, P * u : P * (u + 1)],
                    rhs=z2_w[h][:].bitcast(FP8X4),
                    rhs_scale=z2_s[h][:],
                    start=True,
                    stop=True,
                )
                nc.scalar.activation(s_win[u][:, BANK * h : BANK * (h + 1)], acc[:], ACT.Copy, scale=0.0625)

        out_rows = out_0.rearrange("(p u) w -> p u w", u=4)
        out_words = out_1[0].rearrange("p w t -> p (w t)").bitcast(I32)
        o_s = tile("o_s", [U], U8)
        o_w = tile("o_w", [U], U32)
        starts = [sum(CHUNKS[:c]) for c in range(len(CHUNKS))]

        def fetch_first(dst, c, u):
            nc.vector.tensor_copy(dst, s_win[u][:].indirect(l_n4[:, starts[c] // 16 : (starts[c] + CHUNKS[c]) // 16]))

        def product(dst, c, u, first):
            cols = slice(starts[c], starts[c] + CHUNKS[c])
            nc.vector.tensor_tensor(
                dst[:, u, :], s_win[u][:].indirect(l_n5[:, cols.start // 16 : cols.stop // 16]), first, MULT
            )
            nc.sync.dma_start(out_rows[:, u, cols], dst[:, u, :])

        first_a = [tile(f"first_a{u}", [CHUNKS[0]], F32) for u in range(4)]
        first_b = tile("first_b", [4, CHUNKS[1]], F32)
        prod_a = tile("prod_a", [4, CHUNKS[0]], F32)
        for u in range(4):
            fetch_first(first_a[u][:], 0, u)
            fetch_first(first_b[:, u, :], 1, u)
            product(prod_a, 0, u, first_a[u][:])
        later = sb.tile([P, 2, 4, HALF], F32, name="later", tag="first_a3", align_bytes=64)
        prod_c = tile("prod_c", [4, CHUNKS[2]], F32)
        prod = [prod_a, later[:, 0], prod_c]
        first_c = later[:, 1]

        def regroup(eng_copy, c, a, b):
            o_in = tile(f"o_in{c}_{a}", [b - a, 4], BF16)
            eng_copy(
                o_in[:].rearrange("p (c i) u -> p c u i", i=4), prod[c][:, :, a:b].rearrange("p u (c i) -> p c u i", i=4)
            )
            return o_in

        def quantize_out(o_in, cols):
            nc.vector.quantize_mx(
                out=o_w[:, cols].bitcast(FP8X4), scales=o_s[:, cols], in_=o_in[:].rearrange("p w u -> p (w u)")
            )

        def finish(o_in, c):
            cols = slice(starts[c], starts[c] + CHUNKS[c])
            quantize_out(o_in, cols)
            nc.sync.dma_start(out_words[:, cols], o_w[:, cols].bitcast(I32))

        in_0 = regroup(nc.scalar.copy, 0, 0, CHUNKS[0])
        for u in range(4):
            fetch_first(first_c[:, u, :], 2, u)
            product(prod[1], 1, u, first_b[:, u, :])
        finish(in_0, 0)
        in_1 = regroup(nc.scalar.copy, 1, 0, CHUNKS[1])
        for u in range(4):
            product(prod[2], 2, u, first_c[:, u, :])
        finish(in_1, 1)
        half = CHUNKS[-1] // 2
        in_a = regroup(nc.vector.tensor_copy, len(CHUNKS) - 1, 0, half)
        in_b = regroup(nc.scalar.copy, len(CHUNKS) - 1, half, 2 * half)
        quantize_out(in_a, slice(starts[-1], starts[-1] + half))
        quantize_out(in_b, slice(starts[-1] + half, U))
        nc.scalar.dma_start(out_words[:, starts[-1] :], o_w[:, starts[-1] :].bitcast(I32))
        for q in range(4):
            eng = nc.scalar if q % 2 == 1 else nc.sync
            eng.dma_start(out_2[0, 4 * q : 4 * q + 4, :].bitcast(I32), o_s[32 * q : 32 * q + 4, :].bitcast(I32))
